import numpy as np
import ml_dtypes


def mxq(x, axis, fmt="e4m3"):
    dtype, down = {"e4m3": (ml_dtypes.float8_e4m3fn, 7), "e5m2": (ml_dtypes.float8_e5m2, 14)}[fmt]
    v = np.moveaxis(np.asarray(x, np.float32).astype(ml_dtypes.bfloat16).astype(np.float64), axis, -1)
    blocks = v.reshape(v.shape[:-1] + (-1, 32))
    amax = np.abs(blocks).max(-1, keepdims=True)
    byte = np.maximum(np.where(amax > 0, np.frexp(amax)[1] - 1 + 127, 0) - down, 1)
    scale = np.exp2(byte - 127.0)
    codes = (blocks / scale).astype(np.float32).astype(dtype).astype(np.float64)
    return np.moveaxis((codes * scale).reshape(v.shape), -1, axis)


WIDE = False


def mx_kscale(k):
    if not WIDE:
        return np.ones(k)
    levels = np.array([10, -10, 5, -5, 0])
    if k % 512:
        return np.exp2(np.random.permutation(np.resize(levels, k // 32))).repeat(32)
    a = np.empty((k // 512, 16))
    for p in range(k // 512):
        a[p, :8] = np.random.permutation(np.resize(levels, 8))
        for g in range(8):
            far = levels[np.abs(levels - a[p, g]) >= 10]
            a[p, g + 8] = far[np.random.randint(len(far))]
    return np.exp2(a.ravel()).repeat(32)


def f64(x):
    return np.asarray(x).astype(np.float64)


def striped(idx):
    return np.tile(idx.reshape(-1, 16).T, (8, 1)).astype(np.uint16)


def unstriped(offs):
    return offs[:16].T.reshape(-1).astype(np.int64)


E2M1 = np.array([0.0, 0.5, 1.0, 1.5, 2.0, 3.0, 4.0, 6.0, -0.0, -0.5, -1.0, -1.5, -2.0, -3.0, -4.0, -6.0])


def pack_weight(w, fmt):
    k, n = w.shape
    w = f64(np.asarray(w, np.float32).astype(ml_dtypes.bfloat16)).reshape(k // 32, 32, n)
    amax = np.abs(w).max(1)
    if fmt == "e4m3":
        byte = np.frexp(amax)[1] - 1 + 127 - 7
    else:
        mant, ex = np.frexp(amax / 6.0)
        byte = np.where(mant > 0.5, ex, ex - 1) + 127
    byte = np.clip(np.where(amax > 0, byte, 1), 1, 254)
    scaled = (w * np.exp2(127.0 - byte)[:, None, :]).reshape(k, n).astype(np.float32)
    by_word = np.ascontiguousarray(scaled.reshape(k // 512, 128, 4, n).transpose(0, 1, 3, 2))
    if fmt == "e4m3":
        words = by_word.astype(ml_dtypes.float8_e4m3fn).view(np.uint8)
    else:
        c = by_word.astype(ml_dtypes.float4_e2m1fn).view(np.uint8) & 0xF
        words = (c[..., 0::2] | (c[..., 1::2] << 4)).reshape(k // 512, 128, 2 * n)
    return np.ascontiguousarray(words), np.ascontiguousarray(byte.astype(np.uint8).reshape(k // 512, 16, n))


def unpack_weight(words, scales, fmt):
    g, _, n = scales.shape
    words = np.ascontiguousarray(words).reshape(g, 128, n, -1)
    if fmt == "e4m3":
        vals = words.view(ml_dtypes.float8_e4m3fn).astype(np.float64)
    else:
        nib = np.empty((g, 128, n, 4), np.uint8)
        nib[..., 0::2] = words & 0xF
        nib[..., 1::2] = words >> 4
        vals = E2M1[nib]
    vals = vals * np.repeat(np.exp2(scales.astype(np.float64) - 127.0), 8, axis=1)[..., None]
    return vals.transpose(0, 1, 3, 2).reshape(g * 512, n)


def pack_table(v):
    words, scales = pack_weight(v, "e4m3")
    return np.concatenate([words.reshape(words.shape[0], -1), scales.reshape(scales.shape[0], -1)], axis=1)


def unpack_table(tab):
    g, t = tab.shape[0], tab.shape[1] // 528
    return unpack_weight(tab[:, :512 * t].reshape(g, 128, t, 4), tab[:, 512 * t:].reshape(g, 16, t), "e4m3")


def split(x):
    m, e = np.frexp(f64(x))
    hi = np.ldexp(np.trunc(16.0 * m) / 16.0, e)
    return hi, f64(x) - hi


K, M, T, S = 512, 128, 4096, 1024


def setup_inputs():
    n = np.random.standard_normal
    s = mx_kscale(K)[:, None]
    return {
        "tab": pack_table(n((K, T)) * s),
        "w": (n((K, M)) / np.sqrt(K) / s).astype(np.float32),
        "offs": striped(np.random.permutation(T)[:S]),
    }


def reference(tab, w, offs):
    tab_ = unpack_table(tab)[:, unstriped(offs)]
    w_hi, w_lo = split(w)
    w_hi_, w_lo_ = mxq(w_hi, 0, "e4m3"), mxq(w_lo, 0, "e4m3")
    y = w_hi_.T @ tab_ + w_lo_.T @ tab_
    return y

@@ -1,0 +1,113 @@
+import concourse.mybir as mybir
+
+K, M, T, S = 512, 128, 4096, 1024
+P = 128
+PACK = 4
+LANES = 16
+QUADRANT = 32
+HALF = S // 2
+QUARTER = S // 4
+
+FLOPS = 2 * 2 * K * M * S
+
+F32 = mybir.dt.float32
+BF16 = mybir.dt.bfloat16
+I32 = mybir.dt.int32
+U32 = mybir.dt.uint32
+U16 = mybir.dt.uint16
+U8 = mybir.dt.uint8
+FP8X4 = mybir.dt.float8_e4m3fn_x4
+ALU = mybir.AluOpType
+
+HI_BITS = -(1 << 20)
+
+
+def tile_list_tabw_hl_none_kernel(tc, tab, w, offs, out):
+    nc = tc.nc
+    with (
+        tc.tile_pool(name="keep", bufs=1) as keep,
+        tc.psum_pool(name="psum", bufs=1) as psum,
+    ):
+        offsets = keep.tile([P, S // LANES], U16, name="offsets")
+        w_raw = keep.tile([P, PACK, M], F32, name="w_raw", align_bytes=64)
+        table_words = keep.tile([P, T], I32, name="table_words", align_bytes=64)
+        table_scales = keep.tile([P, T], U8, name="table_scales", align_bytes=64)
+
+        nc.vector.memset(table_scales[:].bitcast(I32), 0)
+
+        nc.sync.dma_start(w_raw[:], w.rearrange("(p j) n -> p j n", j=PACK))
+        nc.sync.dma_start(offsets[:], offs)
+        scale_rows = tab[0, PACK * P * T :].rearrange("(q t) -> q t", t=T)
+        for r in range(4):
+            nc.sync.dma_start(
+                table_scales[r:P:QUADRANT, :].bitcast(I32),
+                scale_rows[r : K // 32 : 4, :].bitcast(I32),
+            )
+        nc.sync.dma_start(
+            table_words[:],
+            tab[0, : PACK * P * T].rearrange("(p b) -> p b", p=P).bitcast(I32),
+        )
+
+        w_hi = keep.tile([P, PACK, M], I32, name="w_hi", align_bytes=64)
+        nc.vector.tensor_scalar(w_hi[:], w_raw[:].bitcast(I32), HI_BITS, None, ALU.bitwise_and)
+        hi_grouped = keep.tile([P, M, PACK], BF16, name="hi_grouped", align_bytes=64)
+        lo_grouped = keep.tile([P, M, PACK], BF16, name="lo_grouped", align_bytes=64)
+        w_hi_f = w_hi[:].bitcast(F32)
+        nc.scalar.copy(hi_grouped[:], w_hi_f.rearrange("p j n -> p n j"))
+        nc.vector.tensor_tensor(
+            lo_grouped[:],
+            w_raw[:].rearrange("p j n -> p n j"),
+            w_hi_f.rearrange("p j n -> p n j"),
+            ALU.subtract,
+        )
+
+        picked_scales = keep.tile([P, S], U8, name="picked_scales", align_bytes=64)
+        nc.vector.tensor_copy(picked_scales[:], table_scales[:].indirect(offsets[:]))
+
+        parts = []
+        for name, grouped in (("lo", lo_grouped), ("hi", hi_grouped)):
+            codes = keep.tile([P, M], U32, name=name + "_codes", align_bytes=64)
+            scales = keep.tile([P, M], U8, name=name + "_scales", align_bytes=64)
+            nc.vector.quantize_mx(
+                out=codes[:].bitcast(FP8X4),
+                scales=scales[:],
+                in_=grouped[:].rearrange("p n j -> p (n j)"),
+            )
+            parts.append((codes, scales))
+
+        words = table_words[:].bitcast(U32)
+        picked = []
+        for h in range(2):
+            picked_words = keep.tile([P, HALF], U32, name="picked_words%d" % h, align_bytes=64)
+            cols = HALF // LANES
+            nc.vector.tensor_copy(picked_words[:], words.indirect(offsets[:, h * cols : (h + 1) * cols]))
+            picked.append(picked_words)
+
+        def product(h, first, width, name):
+            bank = psum.tile([P, width], F32, name="bank_" + name)
+            for i, (codes, scales) in enumerate(parts):
+                nc.tensor.matmul_mx(
+                    out=bank[:],
+                    lhsT=codes[:].bitcast(FP8X4),
+                    lhsT_scale=scales[:],
+                    rhs=picked[h][:, first : first + width].bitcast(FP8X4),
+                    rhs_scale=picked_scales[:, h * HALF + first : h * HALF + first + width],
+                    start=(i == 0),
+                    stop=(i == 1),
+                )
+            return bank
+
+        bank = product(0, 0, HALF, "a")
+        result = keep.tile([P, HALF], F32, name="result_a")
+        nc.scalar.copy(result[:], bank[:])
+        nc.sync.dma_start(out[:, 0:HALF], result[:])
+
+        bank_b = product(1, 0, QUARTER, "b")
+        result_b = keep.tile([P, QUARTER], F32, name="result_b")
+        nc.vector.tensor_copy(result_b[:], bank_b[:])
+        nc.sync.dma_start(out[:, HALF : HALF + QUARTER], result_b[:])
+
+        bank_c = product(1, QUARTER, QUARTER, "c")
+        result_c = keep.tile([P, QUARTER], F32, name="result_c")
+        nc.scalar.copy(result_c[:], bank_c[:])
+        nc.scalar.dma_start(out[:, HALF + QUARTER : S], result_c[:])

@@ -7,6 +7,7 @@ LANES = 16
 QUADRANT = 32
 HALF = S // 2
 QUARTER = S // 4
+FIRST = 1024
 
 FLOPS = 2 * 2 * K * M * S
 
@@ -33,20 +34,20 @@ def tile_list_tabw_hl_none_kernel(tc, tab, w, offs, out):
         table_words = keep.tile([P, T], I32, name="table_words", align_bytes=64)
         table_scales = keep.tile([P, T], U8, name="table_scales", align_bytes=64)
 
-        nc.vector.memset(table_scales[:].bitcast(I32), 0)
-
         nc.sync.dma_start(w_raw[:], w.rearrange("(p j) n -> p j n", j=PACK))
         nc.sync.dma_start(offsets[:], offs)
+        word_rows = tab[0, : PACK * P * T].rearrange("(p b) -> p b", p=P).bitcast(I32)
+        nc.sync.dma_start(table_words[:, :FIRST], word_rows[:, :FIRST])
+
+        nc.vector.memset(table_scales[:].bitcast(I32), 0)
+        nc.vector.memset(table_words[:, T - 8 :], 0)
         scale_rows = tab[0, PACK * P * T :].rearrange("(q t) -> q t", t=T)
         for r in range(4):
             nc.sync.dma_start(
                 table_scales[r:P:QUADRANT, :].bitcast(I32),
                 scale_rows[r : K // 32 : 4, :].bitcast(I32),
             )
-        nc.sync.dma_start(
-            table_words[:],
-            tab[0, : PACK * P * T].rearrange("(p b) -> p b", p=P).bitcast(I32),
-        )
+        nc.sync.dma_start(table_words[:, FIRST:], word_rows[:, FIRST:])
 
         w_hi = keep.tile([P, PACK, M], I32, name="w_hi", align_bytes=64)
         nc.vector.tensor_scalar(w_hi[:], w_raw[:].bitcast(I32), HI_BITS, None, ALU.bitwise_and)
@@ -61,9 +62,6 @@ def tile_list_tabw_hl_none_kernel(tc, tab, w, offs, out):
             ALU.subtract,
         )
 
-        picked_scales = keep.tile([P, S], U8, name="picked_scales", align_bytes=64)
-        nc.vector.tensor_copy(picked_scales[:], table_scales[:].indirect(offsets[:]))
-
         parts = []
         for name, grouped in (("lo", lo_grouped), ("hi", hi_grouped)):
             codes = keep.tile([P, M], U32, name=name + "_codes", align_bytes=64)
@@ -74,6 +72,9 @@ def tile_list_tabw_hl_none_kernel(tc, tab, w, offs, out):
                 in_=grouped[:].rearrange("p n j -> p (n j)"),
             )
             parts.append((codes, scales))
+
+        picked_scales = keep.tile([P, S], U8, name="picked_scales", align_bytes=64)
+        nc.vector.tensor_copy(picked_scales[:], table_scales[:].indirect(offsets[:]))
 
         words = table_words[:].bitcast(U32)
         picked = []

import concourse.mybir as mybir

K, M, T, S = 512, 128, 4096, 1024
P = 128
PACK = 4
LANES = 16
QUADRANT = 32
HALF = S // 2
QUARTER = S // 4
FIRST = 1024

FLOPS = 2 * 2 * K * M * S

F32 = mybir.dt.float32
BF16 = mybir.dt.bfloat16
I32 = mybir.dt.int32
U32 = mybir.dt.uint32
U16 = mybir.dt.uint16
U8 = mybir.dt.uint8
FP8X4 = mybir.dt.float8_e4m3fn_x4
ALU = mybir.AluOpType

HI_BITS = -(1 << 20)


def tile_list_tabw_hl_none_kernel(tc, tab, w, offs, out):
    nc = tc.nc
    with (
        tc.tile_pool(name="keep", bufs=1) as keep,
        tc.psum_pool(name="psum", bufs=1) as psum,
    ):
        offsets = keep.tile([P, S // LANES], U16, name="offsets")
        w_raw = keep.tile([P, PACK, M], F32, name="w_raw", align_bytes=64)
        table_words = keep.tile([P, T], I32, name="table_words", align_bytes=64)
        table_scales = keep.tile([P, T], U8, name="table_scales", align_bytes=64)

        nc.sync.dma_start(w_raw[:], w.rearrange("(p j) n -> p j n", j=PACK))
        nc.sync.dma_start(offsets[:], offs)
        word_rows = tab[0, : PACK * P * T].rearrange("(p b) -> p b", p=P).bitcast(I32)
        nc.sync.dma_start(table_words[:, :FIRST], word_rows[:, :FIRST])

        nc.vector.memset(table_scales[:].bitcast(I32), 0)
        nc.vector.memset(table_words[:, T - 8 :], 0)
        scale_rows = tab[0, PACK * P * T :].rearrange("(q t) -> q t", t=T)
        for r in range(4):
            nc.sync.dma_start(
                table_scales[r:P:QUADRANT, :].bitcast(I32),
                scale_rows[r : K // 32 : 4, :].bitcast(I32),
            )
        nc.sync.dma_start(table_words[:, FIRST:], word_rows[:, FIRST:])

        w_hi = keep.tile([P, PACK, M], I32, name="w_hi", align_bytes=64)
        nc.vector.tensor_scalar(w_hi[:], w_raw[:].bitcast(I32), HI_BITS, None, ALU.bitwise_and)
        hi_grouped = keep.tile([P, M, PACK], BF16, name="hi_grouped", align_bytes=64)
        lo_grouped = keep.tile([P, M, PACK], BF16, name="lo_grouped", align_bytes=64)
        w_hi_f = w_hi[:].bitcast(F32)
        nc.scalar.copy(hi_grouped[:], w_hi_f.rearrange("p j n -> p n j"))
        nc.vector.tensor_tensor(
            lo_grouped[:],
            w_raw[:].rearrange("p j n -> p n j"),
            w_hi_f.rearrange("p j n -> p n j"),
            ALU.subtract,
        )

        parts = []
        for name, grouped in (("lo", lo_grouped), ("hi", hi_grouped)):
            codes = keep.tile([P, M], U32, name=name + "_codes", align_bytes=64)
            scales = keep.tile([P, M], U8, name=name + "_scales", align_bytes=64)
            nc.vector.quantize_mx(
                out=codes[:].bitcast(FP8X4),
                scales=scales[:],
                in_=grouped[:].rearrange("p n j -> p (n j)"),
            )
            parts.append((codes, scales))

        picked_scales = keep.tile([P, S], U8, name="picked_scales", align_bytes=64)
        nc.vector.tensor_copy(picked_scales[:], table_scales[:].indirect(offsets[:]))

        words = table_words[:].bitcast(U32)
        picked = []
        for h in range(2):
            picked_words = keep.tile([P, HALF], U32, name="picked_words%d" % h, align_bytes=64)
            cols = HALF // LANES
            nc.vector.tensor_copy(picked_words[:], words.indirect(offsets[:, h * cols : (h + 1) * cols]))
            picked.append(picked_words)

        def product(h, first, width, name):
            bank = psum.tile([P, width], F32, name="bank_" + name)
            for i, (codes, scales) in enumerate(parts):
                nc.tensor.matmul_mx(
                    out=bank[:],
                    lhsT=codes[:].bitcast(FP8X4),
                    lhsT_scale=scales[:],
                    rhs=picked[h][:, first : first + width].bitcast(FP8X4),
                    rhs_scale=picked_scales[:, h * HALF + first : h * HALF + first + width],
                    start=(i == 0),
                    stop=(i == 1),
                )
            return bank

        bank = product(0, 0, HALF, "a")
        result = keep.tile([P, HALF], F32, name="result_a")
        nc.scalar.copy(result[:], bank[:])
        nc.sync.dma_start(out[:, 0:HALF], result[:])

        bank_b = product(1, 0, QUARTER, "b")
        result_b = keep.tile([P, QUARTER], F32, name="result_b")
        nc.vector.tensor_copy(result_b[:], bank_b[:])
        nc.sync.dma_start(out[:, HALF : HALF + QUARTER], result_b[:])

        bank_c = product(1, QUARTER, QUARTER, "c")
        result_c = keep.tile([P, QUARTER], F32, name="result_c")
        nc.scalar.copy(result_c[:], bank_c[:])
        nc.scalar.dma_start(out[:, HALF + QUARTER : S], result_c[:])
